import numpy as np
import ml_dtypes


def mxq(x, axis, fmt="e4m3"):
    dtype, down = {"e4m3": (ml_dtypes.float8_e4m3fn, 7), "e5m2": (ml_dtypes.float8_e5m2, 14)}[fmt]
    v = np.moveaxis(np.asarray(x, np.float32).astype(ml_dtypes.bfloat16).astype(np.float64), axis, -1)
    blocks = v.reshape(v.shape[:-1] + (-1, 32))
    amax = np.abs(blocks).max(-1, keepdims=True)
    byte = np.maximum(np.where(amax > 0, np.frexp(amax)[1] - 1 + 127, 0) - down, 1)
    scale = np.exp2(byte - 127.0)
    codes = (blocks / scale).astype(np.float32).astype(dtype).astype(np.float64)
    return np.moveaxis((codes * scale).reshape(v.shape), -1, axis)


WIDE = False


def mx_kscale(k):
    if not WIDE:
        return np.ones(k)
    levels = np.array([10, -10, 5, -5, 0])
    if k % 512:
        return np.exp2(np.random.permutation(np.resize(levels, k // 32))).repeat(32)
    a = np.empty((k // 512, 16))
    for p in range(k // 512):
        a[p, :8] = np.random.permutation(np.resize(levels, 8))
        for g in range(8):
            far = levels[np.abs(levels - a[p, g]) >= 10]
            a[p, g + 8] = far[np.random.randint(len(far))]
    return np.exp2(a.ravel()).repeat(32)


def f64(x):
    return np.asarray(x).astype(np.float64)


def striped(idx):
    return np.tile(np.asarray(idx).reshape(-1, 16).T, (8, 1)).astype(np.uint16)


def unstriped(offs):
    return offs[:16].T.reshape(-1).astype(np.int64)


E2M1 = np.array([0.0, 0.5, 1.0, 1.5, 2.0, 3.0, 4.0, 6.0, -0.0, -0.5, -1.0, -1.5, -2.0, -3.0, -4.0, -6.0])


def pack_weight(w, fmt):
    k, n = w.shape
    w = f64(np.asarray(w, np.float32).astype(ml_dtypes.bfloat16)).reshape(k // 32, 32, n)
    amax = np.abs(w).max(1)
    if fmt == "e4m3":
        byte = np.frexp(amax)[1] - 1 + 127 - 7
    else:
        mant, ex = np.frexp(amax / 6.0)
        byte = np.where(mant > 0.5, ex, ex - 1) + 127
    byte = np.clip(np.where(amax > 0, byte, 1), 1, 254)
    scaled = (w * np.exp2(127.0 - byte)[:, None, :]).reshape(k, n).astype(np.float32)
    by_word = np.ascontiguousarray(scaled.reshape(k // 512, 128, 4, n).transpose(0, 1, 3, 2))
    if fmt == "e4m3":
        words = by_word.astype(ml_dtypes.float8_e4m3fn).view(np.uint8)
    else:
        c = by_word.astype(ml_dtypes.float4_e2m1fn).view(np.uint8) & 0xF
        words = (c[..., 0::2] | (c[..., 1::2] << 4)).reshape(k // 512, 128, 2 * n)
    return np.ascontiguousarray(words), np.ascontiguousarray(byte.astype(np.uint8).reshape(k // 512, 16, n))


def unpack_weight(words, scales, fmt):
    g, _, n = scales.shape
    words = np.ascontiguousarray(words).reshape(g, 128, n, -1)
    if fmt == "e4m3":
        vals = words.view(ml_dtypes.float8_e4m3fn).astype(np.float64)
    else:
        nib = np.empty((g, 128, n, 4), np.uint8)
        nib[..., 0::2] = words & 0xF
        nib[..., 1::2] = words >> 4
        vals = E2M1[nib]
    vals = vals * np.repeat(np.exp2(scales.astype(np.float64) - 127.0), 8, axis=1)[..., None]
    return vals.transpose(0, 1, 3, 2).reshape(g * 512, n)


def sigmoid(v):
    return 1.0 / (1.0 + np.exp(-v))


D, K, R, T, I, Q, U = 512, 512, 512, 2048, 512, 128, 1024


def setup_inputs():
    n = np.random.standard_normal
    idx2 = np.random.permutation(U)[:I]
    idx = np.random.permutation(T)[:I]
    fd = mx_kscale(D)
    fk = mx_kscale(K)
    fi = mx_kscale(I)
    keysp = pack_weight(n((D, T)) / fd[:, None], "e4m3")
    tabp = pack_weight(n((K, T)) / fk[:, None], "e4m3")
    return {
        "query": (n((D, Q)) * 0.6 / np.sqrt(D) * fd[:, None]).astype(np.float32),
        "query2": (n((D, Q)) * 1.0 / np.sqrt(D) * fd[:, None]).astype(np.float32),
        "keys_words": keysp[0],
        "keys_scales": keysp[1],
        "tab_words": tabp[0],
        "tab_scales": tabp[1],
        "w1": (n((K, R)) * 1 / np.sqrt(K) * fk[:, None]).astype(np.float32),
        "gtab": (n((R, U))).astype(np.float32),
        "os": (np.random.uniform(4.0, 16.0, (1, I)) * fi).astype(np.float32),
        "vs": (np.random.uniform(0.5, 2.0, (1, I)) / fi).astype(np.float32),
        "offs2": striped(idx2),
        "offs": striped(idx),
    }


def reference(query, query2, keys_words, keys_scales, tab_words, tab_scales, w1, gtab, os, vs, offs2, offs):
    idx2 = unstriped(offs2)
    idx = unstriped(offs)
    keysu = unpack_weight(keys_words, keys_scales, "e4m3")
    tabu = unpack_weight(tab_words, tab_scales, "e4m3")
    queryq = mxq(f64(query), 0, "e4m3")
    keysidxg = keysu[:, idx]
    a = queryq.T @ keysidxg
    query2q = mxq(f64(query2), 0, "e4m3")
    b = query2q.T @ keysidxg
    p = np.exp(a - np.max(a, axis=1, keepdims=True)) * sigmoid(b)
    z = np.sum(p, axis=1, keepdims=True)
    w = p / z
    w1q = mxq(f64(w1), 0, "e4m3")
    tabidxg = tabu[:, idx]
    zh = w1q.T @ tabidxg
    hg = sigmoid(f64(gtab)[:, idx2])
    hv = zh * hg
    wo1 = w * f64(os)
    wt1 = wo1.T
    hw = hv * f64(vs)
    ht1 = hw.T
    wt1q = mxq(wt1, 0, "e4m3")
    ht1q = mxq(ht1, 0, "e4m3")
    o = wt1q.T @ ht1q
    return o

@@ -1,0 +1,210 @@
+from contextlib import ExitStack
+
+import concourse.mybir as mybir
+from concourse.masks import make_identity
+
+F32 = mybir.dt.float32
+BF16 = mybir.dt.bfloat16
+I32 = mybir.dt.int32
+U32 = mybir.dt.uint32
+U16 = mybir.dt.uint16
+U8 = mybir.dt.uint8
+FP8X4 = mybir.dt.float8_e4m3fn_x4
+ACT = mybir.ActivationFunctionType
+ALU = mybir.AluOpType
+AXIS = mybir.AxisListType
+
+P = 128
+PACK = 4
+SLOTS = 512
+TOKENS = 2048
+GATES = 1024
+HIDDEN = 512
+QUERIES = 128
+CHUNKS = HIDDEN // P
+
+FLOPS = 469762048
+
+
+def tile_attend_lrgated_asked_kernel(tc, query, query2, keys_words, keys_scales, tab_words, tab_scales,
+                                      w1, gtab, slot_factor, value_scale, offs2, offs, out):
+    nc = tc.nc
+    with ExitStack() as ctx:
+        lists = ctx.enter_context(tc.tile_pool(name="lists", bufs=1))
+        sb = ctx.enter_context(tc.tile_pool(name="sb", bufs=1))
+        psum = ctx.enter_context(tc.psum_pool(name="psum", bufs=1))
+
+        token_list = lists.tile([P, SLOTS // 16], U16, name="token_list")
+        gate_list = lists.tile([P, SLOTS // 16], U16, name="gate_list")
+        nc.sync.dma_start(token_list[:], offs)
+        nc.sync.dma_start(gate_list[:], offs2)
+
+        def zeroed_plane(zeroing, name):
+            plane = sb.tile([P, TOKENS], U8, name=name, tag=name, align_bytes=64)
+            zeroing.memset(plane[:].bitcast(I32), 0)
+            return plane
+
+        def load_scale_rows(plane, scales):
+            for quad in range(4):
+                nc.scalar.dma_start(plane[32 * quad:32 * quad + 4, :].bitcast(I32),
+                                    scales[0, 4 * quad:4 * quad + 4, :].bitcast(I32))
+
+        def load_words(words, name, tag):
+            pool_words = sb.tile([P, TOKENS], I32, name=name, tag=tag, align_bytes=64)
+            nc.sync.dma_start(pool_words[:], words[0].rearrange("p n t -> p (n t)").bitcast(I32))
+            return pool_words
+
+        def load_rows(rows, name, tag):
+            raw = sb.tile([P, PACK, rows.shape[1]], F32, name=name, tag=tag, align_bytes=64)
+            nc.sync.dma_start(raw[:], rows.rearrange("(p j) w -> p j w", j=PACK))
+            return raw
+
+        def load_gates(c, tag):
+            rows = sb.tile([P, GATES], F32, name=f"gate_pool{c}", tag=tag, align_bytes=64)
+            nc.sync.dma_start(rows[:], gtab[c * P:(c + 1) * P, :])
+            return rows
+
+        def load_slot_columns(queue, row, name, tag):
+            cols = sb.tile([P, PACK], F32, name=name, tag=tag, align_bytes=64)
+            queue.dma_start(cols[:], row.rearrange("o (p j) -> p (o j)", j=PACK))
+            return cols
+
+        key_plane = zeroed_plane(nc.vector, "key_plane")
+        load_scale_rows(key_plane, keys_scales)
+        key_words = load_words(keys_words, "key_words", "key_words")
+        q_raw = [load_rows(query, "q_raw0", "q_raw0")]
+
+        warm = sb.tile([P, 1], F32, name="warm", tag="q_raw1", align_bytes=64)
+        nc.vector.memset(warm[:], 0.0)
+        warm_out = sb.tile([P, 1], F32, name="warm_out", tag="w1_raw", align_bytes=64)
+        nc.scalar.activation(warm_out[:], warm[:], ACT.Exp)
+        q_raw.append(load_rows(query2, "q_raw1", "q_raw1"))
+        w1_raw = load_rows(w1, "w1_raw", "w1_raw")
+
+        ident = sb.tile([P, P], F32, name="ident")
+        make_identity(nc, ident[:])
+        vs_cols = load_slot_columns(nc.gpsimd, value_scale, "vs_cols", "vs_cols")
+        os_cols = load_slot_columns(nc.gpsimd, slot_factor, "os_cols", "os_cols")
+        zero_bias = sb.tile([P, 1], F32, name="zero_bias", tag="gate0", align_bytes=64)
+        nc.gpsimd.memset(zero_bias[:], 0.0)
+        tab_plane = zeroed_plane(nc.vector, "tab_plane")
+        load_scale_rows(tab_plane, tab_scales)
+
+        def gather_bytes(plane, name, tag):
+            got = sb.tile([P, SLOTS], U8, name=name, tag=tag, align_bytes=64)
+            nc.vector.tensor_copy(got[:], plane[:].indirect(token_list[:]))
+            return got
+
+        def gather_words(pool_words, name, tag):
+            got = sb.tile([P, SLOTS], U32, name=name, tag=tag, align_bytes=64)
+            nc.vector.tensor_copy(got[:], pool_words[:].bitcast(U32).indirect(token_list[:]))
+            return got
+
+        def spread_row(cols, tag):
+            bank = psum.tile([P, PACK, P], F32, name=tag + "_row", tag=tag)
+            for j in range(PACK):
+                nc.tensor.transpose(bank[:, j, :], cols[:, j:j + 1].to_broadcast([P, P]), ident[:])
+            return bank
+
+        def mx_tiles(width, name, codes_tag):
+            codes = sb.tile([P, width], U32, name=name + "_codes", tag=codes_tag, align_bytes=64)
+            scales = sb.tile([P, width], U8, name=name + "_scales", tag=name + "_scales", align_bytes=64)
+            return codes, scales
+
+        def quantize_into(codes, scales, grouped):
+            nc.vector.quantize_mx(out=codes.bitcast(FP8X4), scales=scales, in_=grouped)
+
+        def quantize(grouped, width, name):
+            codes, scales = mx_tiles(width, name, name + "_codes")
+            quantize_into(codes[:], scales[:], grouped[:].rearrange("p w j -> p (w j)"))
+            return codes, scales
+
+        def product(acc, lhs, lhs_cols, rhs, rhs_cols):
+            nc.tensor.matmul_mx(out=acc, lhsT=lhs[0][:, lhs_cols].bitcast(FP8X4), lhsT_scale=lhs[1][:, lhs_cols],
+                                rhs=rhs[0][:, rhs_cols].bitcast(FP8X4), rhs_scale=rhs[1][:, rhs_cols],
+                                start=True, stop=True)
+
+        def turn(values, tag, name, grouped):
+            words = values[:].bitcast(F32)
+            turned = psum.tile([P, 2, P], F32, name=name + "_turned", tag=tag)
+            for u in range(2):
+                nc.tensor.transpose(turned[:, u, :], words[:, u:SLOTS // 2:2], ident[:])
+            nc.scalar.copy(grouped.bitcast(F32).rearrange("p (r u) -> p r u", u=2), turned[:].rearrange("p u r -> p r u"))
+
+        key_bytes = gather_bytes(key_plane, "key_bytes", "key_bytes")
+        tab_pool_words = load_words(tab_words, "tab_pool_words", "key_plane")
+        keys = (gather_words(key_words, "key_codes", "key_codes"), key_bytes)
+        gate_pool = [load_gates(0, "key_words")]
+
+        def cast_query(n):
+            grouped = sb.tile([P, QUERIES, PACK], BF16, name=f"q_grouped{n}", tag=f"q_grouped{n}", align_bytes=64)
+            nc.scalar.copy(grouped[:], q_raw[n][:].rearrange("p j w -> p w j"))
+            return quantize(grouped, QUERIES, f"q{n}")
+
+        score = psum.tile([P, SLOTS], F32, name="score", tag="score")
+        product(score[:], cast_query(0), slice(0, QUERIES), keys, slice(0, SLOTS))
+        gate_pool.append(load_gates(1, "q_grouped0"))
+        gate_pool.append(load_gates(2, "q0_codes"))
+        score2 = psum.tile([P, SLOTS], F32, name="score2")
+        product(score2[:], cast_query(1), slice(0, QUERIES), keys, slice(0, SLOTS))
+        gate_pool.append(load_gates(3, "key_bytes"))
+
+        neg_max = sb.tile([P, 1], F32, name="neg_max", tag="asked", align_bytes=64)
+        nc.vector.tensor_reduce(neg_max[:], score[:], AXIS.X, ALU.max, negate=True)
+        expo = sb.tile([P, SLOTS], F32, name="expo", tag="expo", align_bytes=64)
+        nc.scalar.activation(expo[:], score[:], ACT.Exp, bias=neg_max[:])
+        asked = sb.tile([P, SLOTS], F32, name="asked", tag="asked", align_bytes=64)
+        nc.scalar.activation(asked[:], score2[:], ACT.Sigmoid, bias=zero_bias[:])
+
+        vs_bank = spread_row(vs_cols, "score")
+        vs_row = sb.tile([P, P, PACK], F32, name="vs_row", tag="values0", align_bytes=64)
+        nc.scalar.copy(vs_row[:], vs_bank[:].rearrange("p j n -> p n j"))
+        os_bank = spread_row(os_cols, "os_bank")
+
+        tab_bytes = gather_bytes(tab_plane, "tab_bytes", "q1_scales")
+        w1_grouped = sb.tile([P, HIDDEN, PACK], BF16, name="w1_grouped", tag="q1_codes", align_bytes=64)
+        nc.vector.tensor_copy(w1_grouped[:], w1_raw[:].rearrange("p j w -> p w j"))
+        w1_mx = quantize(w1_grouped, HIDDEN, "w1")
+
+        prob = sb.tile([P, SLOTS], F32, name="prob", tag="q1_codes", align_bytes=64)
+        row_sum = sb.tile([P, 1], F32, name="row_sum")
+        nc.vector.scalar_tensor_tensor(prob[:], expo[:], 1.0, asked[:], ALU.mult, ALU.mult, accum_out=row_sum[:])
+        inv_sum = sb.tile([P, 1], F32, name="inv_sum", tag="inv_sum", align_bytes=64)
+        nc.vector.reciprocal(inv_sum[:], row_sum[:])
+        weights = sb.tile([P, SLOTS], BF16, name="weights", align_bytes=64)
+        nc.vector.scalar_tensor_tensor(weights[:].rearrange("p (n j) -> p n j", j=PACK),
+                                       prob[:].rearrange("p (n j) -> p n j", j=PACK), inv_sum[:],
+                                       os_bank[:].rearrange("p j n -> p n j"), ALU.mult, ALU.mult)
+        tab = (gather_words(tab_pool_words, "tab_codes", "q1_codes"), tab_bytes)
+        w_grouped = sb.tile([P, QUERIES, PACK], BF16, name="w_grouped", align_bytes=64)
+        turn(weights, "score", "w", w_grouped[:].rearrange("p w j -> p (w j)"))
+        w_mx = quantize(w_grouped, QUERIES, "w")
+
+        gate_tags = ["gate0", "key_words", "q_grouped0", "q0_codes"]
+        scaled = []
+        for c in range(CHUNKS):
+            hidden = psum.tile([P, SLOTS], F32, name=f"hidden{c}", tag=f"bank{c}")
+            product(hidden[:], w1_mx, slice(c * P, (c + 1) * P), tab, slice(0, SLOTS))
+            zv = sb.tile([P, SLOTS], F32, name=f"zv{c}")
+            nc.vector.tensor_tensor(zv[:], hidden[:], vs_row[:].rearrange("p n j -> p (n j)"), ALU.mult)
+            scaled.append(zv)
+
+        values = []
+        for c in range(CHUNKS):
+            gate = sb.tile([P, SLOTS], F32, name=f"gate{c}", tag=gate_tags[c], align_bytes=64)
+            nc.scalar.activation(gate[:], gate_pool[c][:].indirect(gate_list[:]), ACT.Sigmoid)
+            values.append(sb.tile([P, SLOTS], BF16, name=f"values{c}", tag=f"values{c}", align_bytes=64))
+            nc.vector.tensor_tensor(values[c][:], scaled[c][:], gate[:], ALU.mult)
+
+        h_grouped = sb.tile([P, HIDDEN * PACK], BF16, name="h_grouped", tag="key_bytes", align_bytes=64)
+        h_mx = mx_tiles(HIDDEN, "h", "q0_codes")
+        for c in range(CHUNKS):
+            cols = slice(c * P, (c + 1) * P)
+            grouped = h_grouped[:, c * P * PACK:(c + 1) * P * PACK]
+            turn(values[c], f"bank{c}", f"h{c}", grouped)
+            quantize_into(h_mx[0][:, cols], h_mx[1][:, cols], grouped)
+            acc = psum.tile([P, P], F32, name=f"acc{c}", tag=f"bank{c}")
+            product(acc[:], w_mx, slice(0, QUERIES), h_mx, cols)
+            result = sb.tile([P, P], F32, name=f"result{c}")
+            nc.vector.tensor_copy(result[:], acc[:])
+            nc.sync.dma_start(out[:, cols], result[:])

@@ -1,7 +1,6 @@
 from contextlib import ExitStack
 
 import concourse.mybir as mybir
-from concourse.masks import make_identity
 
 F32 = mybir.dt.float32
 BF16 = mybir.dt.bfloat16
@@ -69,22 +68,24 @@ def tile_attend_lrgated_asked_kernel(tc, query, query2, keys_words, keys_scales,
             queue.dma_start(cols[:], row.rearrange("o (p j) -> p (o j)", j=PACK))
             return cols
 
+        vs_cols = load_slot_columns(nc.scalar, value_scale, "vs_cols", "vs_cols")
         key_plane = zeroed_plane(nc.vector, "key_plane")
         load_scale_rows(key_plane, keys_scales)
         key_words = load_words(keys_words, "key_words", "key_words")
-        q_raw = [load_rows(query, "q_raw0", "q_raw0")]
 
         warm = sb.tile([P, 1], F32, name="warm", tag="q_raw1", align_bytes=64)
         nc.vector.memset(warm[:], 0.0)
         warm_out = sb.tile([P, 1], F32, name="warm_out", tag="w1_raw", align_bytes=64)
         nc.scalar.activation(warm_out[:], warm[:], ACT.Exp)
-        q_raw.append(load_rows(query2, "q_raw1", "q_raw1"))
+
+        ones = sb.tile([P, P], F32, name="ones", tag="q_raw0", align_bytes=64)
+        nc.vector.memset(ones[:], 1.0)
+        ident = sb.tile([P, P], F32, name="ident")
+        nc.gpsimd.affine_select(out=ident[:], in_=ones[:], compare_op=ALU.is_equal, fill=0.0, base=0,
+                                pattern=[[-1, P]], channel_multiplier=1)
+        q_raw = [load_rows(query, "q_raw0", "q_raw0"), load_rows(query2, "q_raw1", "q_raw1")]
         w1_raw = load_rows(w1, "w1_raw", "w1_raw")
 
-        ident = sb.tile([P, P], F32, name="ident")
-        make_identity(nc, ident[:])
-        vs_cols = load_slot_columns(nc.gpsimd, value_scale, "vs_cols", "vs_cols")
-        os_cols = load_slot_columns(nc.gpsimd, slot_factor, "os_cols", "os_cols")
         zero_bias = sb.tile([P, 1], F32, name="zero_bias", tag="gate0", align_bytes=64)
         nc.gpsimd.memset(zero_bias[:], 0.0)
         tab_plane = zeroed_plane(nc.vector, "tab_plane")
@@ -124,17 +125,22 @@ def tile_attend_lrgated_asked_kernel(tc, query, query2, keys_words, keys_scales,
                                 rhs=rhs[0][:, rhs_cols].bitcast(FP8X4), rhs_scale=rhs[1][:, rhs_cols],
                                 start=True, stop=True)
 
-        def turn(values, tag, name, grouped):
+        def turn(values, tag, name, grouped, copy):
             words = values[:].bitcast(F32)
             turned = psum.tile([P, 2, P], F32, name=name + "_turned", tag=tag)
             for u in range(2):
                 nc.tensor.transpose(turned[:, u, :], words[:, u:SLOTS // 2:2], ident[:])
-            nc.scalar.copy(grouped.bitcast(F32).rearrange("p (r u) -> p r u", u=2), turned[:].rearrange("p u r -> p r u"))
+            copy(grouped.bitcast(F32).rearrange("p (r u) -> p r u", u=2), turned[:].rearrange("p u r -> p r u"))
+
+        vs_bank = spread_row(vs_cols, "vs_bank")
+        vs_row = sb.tile([P, P, PACK], F32, name="vs_row", align_bytes=64)
+        nc.vector.tensor_copy(vs_row[:], vs_bank[:].rearrange("p j n -> p n j"))
+        vs_flat = vs_row[:].rearrange("p n j -> p (n j)")
 
         key_bytes = gather_bytes(key_plane, "key_bytes", "key_bytes")
         tab_pool_words = load_words(tab_words, "tab_pool_words", "key_plane")
         keys = (gather_words(key_words, "key_codes", "key_codes"), key_bytes)
-        gate_pool = [load_gates(0, "key_words")]
+        os_cols = load_slot_columns(nc.scalar, slot_factor, "os_cols", "key_words")
 
         def cast_query(n):
             grouped = sb.tile([P, QUERIES, PACK], BF16, name=f"q_grouped{n}", tag=f"q_grouped{n}", align_bytes=64)
@@ -143,11 +149,10 @@ def tile_attend_lrgated_asked_kernel(tc, query, query2, keys_words, keys_scales,
 
         score = psum.tile([P, SLOTS], F32, name="score", tag="score")
         product(score[:], cast_query(0), slice(0, QUERIES), keys, slice(0, SLOTS))
-        gate_pool.append(load_gates(1, "q_grouped0"))
-        gate_pool.append(load_gates(2, "q0_codes"))
-        score2 = psum.tile([P, SLOTS], F32, name="score2")
+        score2 = psum.tile([P, SLOTS], F32, name="score2", tag="score2")
         product(score2[:], cast_query(1), slice(0, QUERIES), keys, slice(0, SLOTS))
-        gate_pool.append(load_gates(3, "key_bytes"))
+        pool_tags = ["q_grouped0", "q0_codes", "q0_scales", "key_bytes"]
+        gate_pool = [load_gates(c, pool_tags[c]) for c in range(CHUNKS)]
 
         neg_max = sb.tile([P, 1], F32, name="neg_max", tag="asked", align_bytes=64)
         nc.vector.tensor_reduce(neg_max[:], score[:], AXIS.X, ALU.max, negate=True)
@@ -156,17 +161,19 @@ def tile_attend_lrgated_asked_kernel(tc, query, query2, keys_words, keys_scales,
         asked = sb.tile([P, SLOTS], F32, name="asked", tag="asked", align_bytes=64)
         nc.scalar.activation(asked[:], score2[:], ACT.Sigmoid, bias=zero_bias[:])
 
-        vs_bank = spread_row(vs_cols, "score")
-        vs_row = sb.tile([P, P, PACK], F32, name="vs_row", tag="values0", align_bytes=64)
-        nc.scalar.copy(vs_row[:], vs_bank[:].rearrange("p j n -> p n j"))
-        os_bank = spread_row(os_cols, "os_bank")
-
+        os_bank = spread_row(os_cols, "score")
         tab_bytes = gather_bytes(tab_plane, "tab_bytes", "q1_scales")
-        w1_grouped = sb.tile([P, HIDDEN, PACK], BF16, name="w1_grouped", tag="q1_codes", align_bytes=64)
-        nc.vector.tensor_copy(w1_grouped[:], w1_raw[:].rearrange("p j w -> p w j"))
-        w1_mx = quantize(w1_grouped, HIDDEN, "w1")
+        tab = (gather_words(tab_pool_words, "tab_codes", "key_codes"), tab_bytes)
 
-        prob = sb.tile([P, SLOTS], F32, name="prob", tag="q1_codes", align_bytes=64)
+        w1_grouped = sb.tile([P, HIDDEN, PACK], BF16, name="w1_grouped", align_bytes=64)
+        for c in range(CHUNKS):
+            cols = slice(c * P, (c + 1) * P)
+            nc.gpsimd.tensor_scalar(w1_grouped[:, cols, :], w1_raw[:, :, cols].rearrange("p j w -> p w j"),
+                                    1.0, 0.0, ALU.mult, ALU.add)
+        w1_mx = mx_tiles(HIDDEN, "w1", "q1_codes")
+        quantize_into(w1_mx[0][:], w1_mx[1][:], w1_grouped[:].rearrange("p w j -> p (w j)"))
+
+        prob = sb.tile([P, SLOTS], F32, name="prob", tag="prob", align_bytes=64)
         row_sum = sb.tile([P, 1], F32, name="row_sum")
         nc.vector.scalar_tensor_tensor(prob[:], expo[:], 1.0, asked[:], ALU.mult, ALU.mult, accum_out=row_sum[:])
         inv_sum = sb.tile([P, 1], F32, name="inv_sum", tag="inv_sum", align_bytes=64)
@@ -175,36 +182,43 @@ def tile_attend_lrgated_asked_kernel(tc, query, query2, keys_words, keys_scales,
         nc.vector.scalar_tensor_tensor(weights[:].rearrange("p (n j) -> p n j", j=PACK),
                                        prob[:].rearrange("p (n j) -> p n j", j=PACK), inv_sum[:],
                                        os_bank[:].rearrange("p j n -> p n j"), ALU.mult, ALU.mult)
-        tab = (gather_words(tab_pool_words, "tab_codes", "q1_codes"), tab_bytes)
         w_grouped = sb.tile([P, QUERIES, PACK], BF16, name="w_grouped", align_bytes=64)
-        turn(weights, "score", "w", w_grouped[:].rearrange("p w j -> p (w j)"))
+        turn(weights, "vs_bank", "w", w_grouped[:].rearrange("p w j -> p (w j)"), nc.vector.tensor_copy)
         w_mx = quantize(w_grouped, QUERIES, "w")
 
-        gate_tags = ["gate0", "key_words", "q_grouped0", "q0_codes"]
-        scaled = []
+        gate_tags = ["gate0"] + pool_tags[:CHUNKS - 1]
+        hidden = []
         for c in range(CHUNKS):
-            hidden = psum.tile([P, SLOTS], F32, name=f"hidden{c}", tag=f"bank{c}")
-            product(hidden[:], w1_mx, slice(c * P, (c + 1) * P), tab, slice(0, SLOTS))
-            zv = sb.tile([P, SLOTS], F32, name=f"zv{c}")
-            nc.vector.tensor_tensor(zv[:], hidden[:], vs_row[:].rearrange("p n j -> p (n j)"), ALU.mult)
-            scaled.append(zv)
+            hidden.append(psum.tile([P, SLOTS], F32, name=f"hidden{c}", tag=f"bank{c}"))
+            product(hidden[c][:], w1_mx, slice(c * P, (c + 1) * P), tab, slice(0, SLOTS))
+        EARLY = 2
+        scaled_hidden = {}
+        for c in range(EARLY, CHUNKS):
+            scaled_hidden[c] = sb.tile([P, SLOTS], F32, name=f"scaled_hidden{c}")
+            nc.vector.tensor_tensor(scaled_hidden[c][:], hidden[c][:], vs_flat, ALU.mult)
 
         values = []
         for c in range(CHUNKS):
             gate = sb.tile([P, SLOTS], F32, name=f"gate{c}", tag=gate_tags[c], align_bytes=64)
             nc.scalar.activation(gate[:], gate_pool[c][:].indirect(gate_list[:]), ACT.Sigmoid)
-            values.append(sb.tile([P, SLOTS], BF16, name=f"values{c}", tag=f"values{c}", align_bytes=64))
-            nc.vector.tensor_tensor(values[c][:], scaled[c][:], gate[:], ALU.mult)
+            if c < EARLY:
+                scaled_gate = sb.tile([P, SLOTS], F32, name=f"scaled_gate{c}", tag=f"scaled_gate{c}", align_bytes=64)
+                nc.gpsimd.tensor_tensor(scaled_gate[:], gate[:], vs_flat, ALU.mult)
+                values.append(sb.tile([P, SLOTS], BF16, name=f"values{c}", align_bytes=64))
+                nc.vector.tensor_tensor(values[c][:], hidden[c][:], scaled_gate[:], ALU.mult)
+            else:
+                values.append(sb.tile([P, SLOTS], BF16, name=f"values{c}", tag=f"scaled_gate{c - EARLY}", align_bytes=64))
+                nc.vector.tensor_tensor(values[c][:], scaled_hidden[c][:], gate[:], ALU.mult)
 
         h_grouped = sb.tile([P, HIDDEN * PACK], BF16, name="h_grouped", tag="key_bytes", align_bytes=64)
-        h_mx = mx_tiles(HIDDEN, "h", "q0_codes")
-        for c in range(CHUNKS):
-            cols = slice(c * P, (c + 1) * P)
-            grouped = h_grouped[:, c * P * PACK:(c + 1) * P * PACK]
-            turn(values[c], f"bank{c}", f"h{c}", grouped)
-            quantize_into(h_mx[0][:, cols], h_mx[1][:, cols], grouped)
-            acc = psum.tile([P, P], F32, name=f"acc{c}", tag=f"bank{c}")
+        h_mx = mx_tiles(HIDDEN, "h", "q0_scales")
+        for half in range(2):
+            for c in (2 * half, 2 * half + 1):
+                turn(values[c], f"bank{c}", f"h{c}", h_grouped[:, c * P * PACK:(c + 1) * P * PACK], nc.scalar.copy)
+            cols = slice(half * 2 * P, (half + 1) * 2 * P)
+            quantize_into(h_mx[0][:, cols], h_mx[1][:, cols], h_grouped[:, cols.start * PACK:cols.stop * PACK])
+            acc = psum.tile([P, 2 * P], F32, name=f"acc{half}", tag=f"bank{2 * half}")
             product(acc[:], w_mx, slice(0, QUERIES), h_mx, cols)
-            result = sb.tile([P, P], F32, name=f"result{c}")
-            nc.vector.tensor_copy(result[:], acc[:])
+            result = sb.tile([P, 2 * P], F32, name=f"result{half}")
+            nc.scalar.copy(result[:], acc[:])
             nc.sync.dma_start(out[:, cols], result[:])

@@ -1,6 +1,7 @@
 from contextlib import ExitStack
 
 import concourse.mybir as mybir
+from concourse.masks import make_identity
 
 F32 = mybir.dt.float32
 BF16 = mybir.dt.bfloat16
@@ -69,23 +70,21 @@ def tile_attend_lrgated_asked_kernel(tc, query, query2, keys_words, keys_scales,
             return cols
 
         vs_cols = load_slot_columns(nc.scalar, value_scale, "vs_cols", "vs_cols")
-        key_plane = zeroed_plane(nc.vector, "key_plane")
-        load_scale_rows(key_plane, keys_scales)
-        key_words = load_words(keys_words, "key_words", "key_words")
-
+        os_cols = load_slot_columns(nc.scalar, slot_factor, "os_cols", "os_cols")
         warm = sb.tile([P, 1], F32, name="warm", tag="q_raw1", align_bytes=64)
         nc.vector.memset(warm[:], 0.0)
         warm_out = sb.tile([P, 1], F32, name="warm_out", tag="w1_raw", align_bytes=64)
         nc.scalar.activation(warm_out[:], warm[:], ACT.Exp)
+        key_plane = zeroed_plane(nc.vector, "key_plane")
+        load_scale_rows(key_plane, keys_scales)
+        key_words = load_words(keys_words, "key_words", "key_words")
+        q_raw = [load_rows(query, "q_raw0", "q_raw0")]
 
-        ones = sb.tile([P, P], F32, name="ones", tag="q_raw0", align_bytes=64)
-        nc.vector.memset(ones[:], 1.0)
-        ident = sb.tile([P, P], F32, name="ident")
-        nc.gpsimd.affine_select(out=ident[:], in_=ones[:], compare_op=ALU.is_equal, fill=0.0, base=0,
-                                pattern=[[-1, P]], channel_multiplier=1)
-        q_raw = [load_rows(query, "q_raw0", "q_raw0"), load_rows(query2, "q_raw1", "q_raw1")]
+        q_raw.append(load_rows(query2, "q_raw1", "q_raw1"))
         w1_raw = load_rows(w1, "w1_raw", "w1_raw")
 
+        ident = sb.tile([P, P], F32, name="ident")
+        make_identity(nc, ident[:])
         zero_bias = sb.tile([P, 1], F32, name="zero_bias", tag="gate0", align_bytes=64)
         nc.gpsimd.memset(zero_bias[:], 0.0)
         tab_plane = zeroed_plane(nc.vector, "tab_plane")
@@ -136,11 +135,10 @@ def tile_attend_lrgated_asked_kernel(tc, query, query2, keys_words, keys_scales,
         vs_row = sb.tile([P, P, PACK], F32, name="vs_row", align_bytes=64)
         nc.vector.tensor_copy(vs_row[:], vs_bank[:].rearrange("p j n -> p n j"))
         vs_flat = vs_row[:].rearrange("p n j -> p (n j)")
+        os_bank = spread_row(os_cols, "os_bank")
 
-        key_bytes = gather_bytes(key_plane, "key_bytes", "key_bytes")
-        tab_pool_words = load_words(tab_words, "tab_pool_words", "key_plane")
-        keys = (gather_words(key_words, "key_codes", "key_codes"), key_bytes)
-        os_cols = load_slot_columns(nc.scalar, slot_factor, "os_cols", "key_words")
+        key_codes = gather_words(key_words, "key_codes", "key_codes")
+        keys = (key_codes, gather_bytes(key_plane, "key_bytes", "key_words"))
 
         def cast_query(n):
             grouped = sb.tile([P, QUERIES, PACK], BF16, name=f"q_grouped{n}", tag=f"q_grouped{n}", align_bytes=64)
@@ -149,9 +147,10 @@ def tile_attend_lrgated_asked_kernel(tc, query, query2, keys_words, keys_scales,
 
         score = psum.tile([P, SLOTS], F32, name="score", tag="score")
         product(score[:], cast_query(0), slice(0, QUERIES), keys, slice(0, SLOTS))
+        tab_pool_words = load_words(tab_words, "tab_pool_words", "q_raw0")
         score2 = psum.tile([P, SLOTS], F32, name="score2", tag="score2")
         product(score2[:], cast_query(1), slice(0, QUERIES), keys, slice(0, SLOTS))
-        pool_tags = ["q_grouped0", "q0_codes", "q0_scales", "key_bytes"]
+        pool_tags = ["q_grouped0", "q0_codes", "q0_scales", "key_words"]
         gate_pool = [load_gates(c, pool_tags[c]) for c in range(CHUNKS)]
 
         neg_max = sb.tile([P, 1], F32, name="neg_max", tag="asked", align_bytes=64)
@@ -161,7 +160,6 @@ def tile_attend_lrgated_asked_kernel(tc, query, query2, keys_words, keys_scales,
         asked = sb.tile([P, SLOTS], F32, name="asked", tag="asked", align_bytes=64)
         nc.scalar.activation(asked[:], score2[:], ACT.Sigmoid, bias=zero_bias[:])
 
-        os_bank = spread_row(os_cols, "score")
         tab_bytes = gather_bytes(tab_plane, "tab_bytes", "q1_scales")
         tab = (gather_words(tab_pool_words, "tab_codes", "key_codes"), tab_bytes)
 
@@ -200,7 +198,12 @@ def tile_attend_lrgated_asked_kernel(tc, query, query2, keys_words, keys_scales,
         values = []
         for c in range(CHUNKS):
             gate = sb.tile([P, SLOTS], F32, name=f"gate{c}", tag=gate_tags[c], align_bytes=64)
-            nc.scalar.activation(gate[:], gate_pool[c][:].indirect(gate_list[:]), ACT.Sigmoid)
+            pieces = 2 if c == CHUNKS - 1 else 1
+            width = SLOTS // pieces
+            for piece in range(pieces):
+                nc.scalar.activation(gate[:, piece * width:(piece + 1) * width],
+                                     gate_pool[c][:].indirect(gate_list[:, piece * width // 16:(piece + 1) * width // 16]),
+                                     ACT.Sigmoid)
             if c < EARLY:
                 scaled_gate = sb.tile([P, SLOTS], F32, name=f"scaled_gate{c}", tag=f"scaled_gate{c}", align_bytes=64)
                 nc.gpsimd.tensor_tensor(scaled_gate[:], gate[:], vs_flat, ALU.mult)
@@ -208,17 +211,19 @@ def tile_attend_lrgated_asked_kernel(tc, query, query2, keys_words, keys_scales,
                 nc.vector.tensor_tensor(values[c][:], hidden[c][:], scaled_gate[:], ALU.mult)
             else:
                 values.append(sb.tile([P, SLOTS], BF16, name=f"values{c}", tag=f"scaled_gate{c - EARLY}", align_bytes=64))
-                nc.vector.tensor_tensor(values[c][:], scaled_hidden[c][:], gate[:], ALU.mult)
+                for piece in range(pieces):
+                    slots = slice(piece * width, (piece + 1) * width)
+                    nc.vector.tensor_tensor(values[c][:, slots], scaled_hidden[c][:, slots], gate[:, slots], ALU.mult)
 
-        h_grouped = sb.tile([P, HIDDEN * PACK], BF16, name="h_grouped", tag="key_bytes", align_bytes=64)
+        h_grouped = sb.tile([P, HIDDEN * PACK], BF16, name="h_grouped", tag="key_words", align_bytes=64)
         h_mx = mx_tiles(HIDDEN, "h", "q0_scales")
-        for half in range(2):
-            for c in (2 * half, 2 * half + 1):
-                turn(values[c], f"bank{c}", f"h{c}", h_grouped[:, c * P * PACK:(c + 1) * P * PACK], nc.scalar.copy)
-            cols = slice(half * 2 * P, (half + 1) * 2 * P)
+        for c in range(CHUNKS):
+            turn(values[c], f"bank{c}", f"h{c}", h_grouped[:, c * P * PACK:(c + 1) * P * PACK], nc.scalar.copy)
+        for first, count in ((0, 2), (2, 1), (3, 1)):
+            cols = slice(first * P, (first + count) * P)
             quantize_into(h_mx[0][:, cols], h_mx[1][:, cols], h_grouped[:, cols.start * PACK:cols.stop * PACK])
-            acc = psum.tile([P, 2 * P], F32, name=f"acc{half}", tag=f"bank{2 * half}")
+            acc = psum.tile([P, count * P], F32, name=f"acc{first}", tag=f"bank{first}")
             product(acc[:], w_mx, slice(0, QUERIES), h_mx, cols)
-            result = sb.tile([P, 2 * P], F32, name=f"result{half}")
+            result = sb.tile([P, count * P], F32, name=f"result{first}")
             nc.scalar.copy(result[:], acc[:])
             nc.sync.dma_start(out[:, cols], result[:])

from contextlib import ExitStack

import concourse.mybir as mybir
from concourse.masks import make_identity

F32 = mybir.dt.float32
BF16 = mybir.dt.bfloat16
I32 = mybir.dt.int32
U32 = mybir.dt.uint32
U16 = mybir.dt.uint16
U8 = mybir.dt.uint8
FP8X4 = mybir.dt.float8_e4m3fn_x4
ACT = mybir.ActivationFunctionType
ALU = mybir.AluOpType
AXIS = mybir.AxisListType

P = 128
PACK = 4
SLOTS = 512
TOKENS = 2048
GATES = 1024
HIDDEN = 512
QUERIES = 128
CHUNKS = HIDDEN // P

FLOPS = 469762048


def tile_attend_lrgated_asked_kernel(tc, query, query2, keys_words, keys_scales, tab_words, tab_scales,
                                      w1, gtab, slot_factor, value_scale, offs2, offs, out):
    nc = tc.nc
    with ExitStack() as ctx:
        lists = ctx.enter_context(tc.tile_pool(name="lists", bufs=1))
        sb = ctx.enter_context(tc.tile_pool(name="sb", bufs=1))
        psum = ctx.enter_context(tc.psum_pool(name="psum", bufs=1))

        token_list = lists.tile([P, SLOTS // 16], U16, name="token_list")
        gate_list = lists.tile([P, SLOTS // 16], U16, name="gate_list")
        nc.sync.dma_start(token_list[:], offs)
        nc.sync.dma_start(gate_list[:], offs2)

        def zeroed_plane(zeroing, name):
            plane = sb.tile([P, TOKENS], U8, name=name, tag=name, align_bytes=64)
            zeroing.memset(plane[:].bitcast(I32), 0)
            return plane

        def load_scale_rows(plane, scales):
            for quad in range(4):
                nc.scalar.dma_start(plane[32 * quad:32 * quad + 4, :].bitcast(I32),
                                    scales[0, 4 * quad:4 * quad + 4, :].bitcast(I32))

        def load_words(words, name, tag):
            pool_words = sb.tile([P, TOKENS], I32, name=name, tag=tag, align_bytes=64)
            nc.sync.dma_start(pool_words[:], words[0].rearrange("p n t -> p (n t)").bitcast(I32))
            return pool_words

        def load_rows(rows, name, tag):
            raw = sb.tile([P, PACK, rows.shape[1]], F32, name=name, tag=tag, align_bytes=64)
            nc.sync.dma_start(raw[:], rows.rearrange("(p j) w -> p j w", j=PACK))
            return raw

        def load_gates(c, tag):
            rows = sb.tile([P, GATES], F32, name=f"gate_pool{c}", tag=tag, align_bytes=64)
            nc.sync.dma_start(rows[:], gtab[c * P:(c + 1) * P, :])
            return rows

        def load_slot_columns(queue, row, name, tag):
            cols = sb.tile([P, PACK], F32, name=name, tag=tag, align_bytes=64)
            queue.dma_start(cols[:], row.rearrange("o (p j) -> p (o j)", j=PACK))
            return cols

        vs_cols = load_slot_columns(nc.scalar, value_scale, "vs_cols", "vs_cols")
        os_cols = load_slot_columns(nc.scalar, slot_factor, "os_cols", "os_cols")
        warm = sb.tile([P, 1], F32, name="warm", tag="q_raw1", align_bytes=64)
        nc.vector.memset(warm[:], 0.0)
        warm_out = sb.tile([P, 1], F32, name="warm_out", tag="w1_raw", align_bytes=64)
        nc.scalar.activation(warm_out[:], warm[:], ACT.Exp)
        key_plane = zeroed_plane(nc.vector, "key_plane")
        load_scale_rows(key_plane, keys_scales)
        key_words = load_words(keys_words, "key_words", "key_words")
        q_raw = [load_rows(query, "q_raw0", "q_raw0")]

        q_raw.append(load_rows(query2, "q_raw1", "q_raw1"))
        w1_raw = load_rows(w1, "w1_raw", "w1_raw")

        ident = sb.tile([P, P], F32, name="ident")
        make_identity(nc, ident[:])
        zero_bias = sb.tile([P, 1], F32, name="zero_bias", tag="gate0", align_bytes=64)
        nc.gpsimd.memset(zero_bias[:], 0.0)
        tab_plane = zeroed_plane(nc.vector, "tab_plane")
        load_scale_rows(tab_plane, tab_scales)

        def gather_bytes(plane, name, tag):
            got = sb.tile([P, SLOTS], U8, name=name, tag=tag, align_bytes=64)
            nc.vector.tensor_copy(got[:], plane[:].indirect(token_list[:]))
            return got

        def gather_words(pool_words, name, tag):
            got = sb.tile([P, SLOTS], U32, name=name, tag=tag, align_bytes=64)
            nc.vector.tensor_copy(got[:], pool_words[:].bitcast(U32).indirect(token_list[:]))
            return got

        def spread_row(cols, tag):
            bank = psum.tile([P, PACK, P], F32, name=tag + "_row", tag=tag)
            for j in range(PACK):
                nc.tensor.transpose(bank[:, j, :], cols[:, j:j + 1].to_broadcast([P, P]), ident[:])
            return bank

        def mx_tiles(width, name, codes_tag):
            codes = sb.tile([P, width], U32, name=name + "_codes", tag=codes_tag, align_bytes=64)
            scales = sb.tile([P, width], U8, name=name + "_scales", tag=name + "_scales", align_bytes=64)
            return codes, scales

        def quantize_into(codes, scales, grouped):
            nc.vector.quantize_mx(out=codes.bitcast(FP8X4), scales=scales, in_=grouped)

        def quantize(grouped, width, name):
            codes, scales = mx_tiles(width, name, name + "_codes")
            quantize_into(codes[:], scales[:], grouped[:].rearrange("p w j -> p (w j)"))
            return codes, scales

        def product(acc, lhs, lhs_cols, rhs, rhs_cols):
            nc.tensor.matmul_mx(out=acc, lhsT=lhs[0][:, lhs_cols].bitcast(FP8X4), lhsT_scale=lhs[1][:, lhs_cols],
                                rhs=rhs[0][:, rhs_cols].bitcast(FP8X4), rhs_scale=rhs[1][:, rhs_cols],
                                start=True, stop=True)

        def turn(values, tag, name, grouped, copy):
            words = values[:].bitcast(F32)
            turned = psum.tile([P, 2, P], F32, name=name + "_turned", tag=tag)
            for u in range(2):
                nc.tensor.transpose(turned[:, u, :], words[:, u:SLOTS // 2:2], ident[:])
            copy(grouped.bitcast(F32).rearrange("p (r u) -> p r u", u=2), turned[:].rearrange("p u r -> p r u"))

        vs_bank = spread_row(vs_cols, "vs_bank")
        vs_row = sb.tile([P, P, PACK], F32, name="vs_row", align_bytes=64)
        nc.vector.tensor_copy(vs_row[:], vs_bank[:].rearrange("p j n -> p n j"))
        vs_flat = vs_row[:].rearrange("p n j -> p (n j)")
        os_bank = spread_row(os_cols, "os_bank")

        key_codes = gather_words(key_words, "key_codes", "key_codes")
        keys = (key_codes, gather_bytes(key_plane, "key_bytes", "key_words"))

        def cast_query(n):
            grouped = sb.tile([P, QUERIES, PACK], BF16, name=f"q_grouped{n}", tag=f"q_grouped{n}", align_bytes=64)
            nc.scalar.copy(grouped[:], q_raw[n][:].rearrange("p j w -> p w j"))
            return quantize(grouped, QUERIES, f"q{n}")

        score = psum.tile([P, SLOTS], F32, name="score", tag="score")
        product(score[:], cast_query(0), slice(0, QUERIES), keys, slice(0, SLOTS))
        tab_pool_words = load_words(tab_words, "tab_pool_words", "q_raw0")
        score2 = psum.tile([P, SLOTS], F32, name="score2", tag="score2")
        product(score2[:], cast_query(1), slice(0, QUERIES), keys, slice(0, SLOTS))
        pool_tags = ["q_grouped0", "q0_codes", "q0_scales", "key_words"]
        gate_pool = [load_gates(c, pool_tags[c]) for c in range(CHUNKS)]

        neg_max = sb.tile([P, 1], F32, name="neg_max", tag="asked", align_bytes=64)
        nc.vector.tensor_reduce(neg_max[:], score[:], AXIS.X, ALU.max, negate=True)
        expo = sb.tile([P, SLOTS], F32, name="expo", tag="expo", align_bytes=64)
        nc.scalar.activation(expo[:], score[:], ACT.Exp, bias=neg_max[:])
        asked = sb.tile([P, SLOTS], F32, name="asked", tag="asked", align_bytes=64)
        nc.scalar.activation(asked[:], score2[:], ACT.Sigmoid, bias=zero_bias[:])

        tab_bytes = gather_bytes(tab_plane, "tab_bytes", "q1_scales")
        tab = (gather_words(tab_pool_words, "tab_codes", "key_codes"), tab_bytes)

        w1_grouped = sb.tile([P, HIDDEN, PACK], BF16, name="w1_grouped", align_bytes=64)
        for c in range(CHUNKS):
            cols = slice(c * P, (c + 1) * P)
            nc.gpsimd.tensor_scalar(w1_grouped[:, cols, :], w1_raw[:, :, cols].rearrange("p j w -> p w j"),
                                    1.0, 0.0, ALU.mult, ALU.add)
        w1_mx = mx_tiles(HIDDEN, "w1", "q1_codes")
        quantize_into(w1_mx[0][:], w1_mx[1][:], w1_grouped[:].rearrange("p w j -> p (w j)"))

        prob = sb.tile([P, SLOTS], F32, name="prob", tag="prob", align_bytes=64)
        row_sum = sb.tile([P, 1], F32, name="row_sum")
        nc.vector.scalar_tensor_tensor(prob[:], expo[:], 1.0, asked[:], ALU.mult, ALU.mult, accum_out=row_sum[:])
        inv_sum = sb.tile([P, 1], F32, name="inv_sum", tag="inv_sum", align_bytes=64)
        nc.vector.reciprocal(inv_sum[:], row_sum[:])
        weights = sb.tile([P, SLOTS], BF16, name="weights", align_bytes=64)
        nc.vector.scalar_tensor_tensor(weights[:].rearrange("p (n j) -> p n j", j=PACK),
                                       prob[:].rearrange("p (n j) -> p n j", j=PACK), inv_sum[:],
                                       os_bank[:].rearrange("p j n -> p n j"), ALU.mult, ALU.mult)
        w_grouped = sb.tile([P, QUERIES, PACK], BF16, name="w_grouped", align_bytes=64)
        turn(weights, "vs_bank", "w", w_grouped[:].rearrange("p w j -> p (w j)"), nc.vector.tensor_copy)
        w_mx = quantize(w_grouped, QUERIES, "w")

        gate_tags = ["gate0"] + pool_tags[:CHUNKS - 1]
        hidden = []
        for c in range(CHUNKS):
            hidden.append(psum.tile([P, SLOTS], F32, name=f"hidden{c}", tag=f"bank{c}"))
            product(hidden[c][:], w1_mx, slice(c * P, (c + 1) * P), tab, slice(0, SLOTS))
        EARLY = 2
        scaled_hidden = {}
        for c in range(EARLY, CHUNKS):
            scaled_hidden[c] = sb.tile([P, SLOTS], F32, name=f"scaled_hidden{c}")
            nc.vector.tensor_tensor(scaled_hidden[c][:], hidden[c][:], vs_flat, ALU.mult)

        values = []
        for c in range(CHUNKS):
            gate = sb.tile([P, SLOTS], F32, name=f"gate{c}", tag=gate_tags[c], align_bytes=64)
            pieces = 2 if c == CHUNKS - 1 else 1
            width = SLOTS // pieces
            for piece in range(pieces):
                nc.scalar.activation(gate[:, piece * width:(piece + 1) * width],
                                     gate_pool[c][:].indirect(gate_list[:, piece * width // 16:(piece + 1) * width // 16]),
                                     ACT.Sigmoid)
            if c < EARLY:
                scaled_gate = sb.tile([P, SLOTS], F32, name=f"scaled_gate{c}", tag=f"scaled_gate{c}", align_bytes=64)
                nc.gpsimd.tensor_tensor(scaled_gate[:], gate[:], vs_flat, ALU.mult)
                values.append(sb.tile([P, SLOTS], BF16, name=f"values{c}", align_bytes=64))
                nc.vector.tensor_tensor(values[c][:], hidden[c][:], scaled_gate[:], ALU.mult)
            else:
                values.append(sb.tile([P, SLOTS], BF16, name=f"values{c}", tag=f"scaled_gate{c - EARLY}", align_bytes=64))
                for piece in range(pieces):
                    slots = slice(piece * width, (piece + 1) * width)
                    nc.vector.tensor_tensor(values[c][:, slots], scaled_hidden[c][:, slots], gate[:, slots], ALU.mult)

        h_grouped = sb.tile([P, HIDDEN * PACK], BF16, name="h_grouped", tag="key_words", align_bytes=64)
        h_mx = mx_tiles(HIDDEN, "h", "q0_scales")
        for c in range(CHUNKS):
            turn(values[c], f"bank{c}", f"h{c}", h_grouped[:, c * P * PACK:(c + 1) * P * PACK], nc.scalar.copy)
        for first, count in ((0, 2), (2, 1), (3, 1)):
            cols = slice(first * P, (first + count) * P)
            quantize_into(h_mx[0][:, cols], h_mx[1][:, cols], h_grouped[:, cols.start * PACK:cols.stop * PACK])
            acc = psum.tile([P, count * P], F32, name=f"acc{first}", tag=f"bank{first}")
            product(acc[:], w_mx, slice(0, QUERIES), h_mx, cols)
            result = sb.tile([P, count * P], F32, name=f"result{first}")
            nc.scalar.copy(result[:], acc[:])
            nc.sync.dma_start(out[:, cols], result[:])
